import numpy as np
import ml_dtypes


def mxq(x, axis, fmt="e4m3"):
    dtype, down = {"e4m3": (ml_dtypes.float8_e4m3fn, 7), "e5m2": (ml_dtypes.float8_e5m2, 14)}[fmt]
    v = np.moveaxis(np.asarray(x, np.float32).astype(ml_dtypes.bfloat16).astype(np.float64), axis, -1)
    blocks = v.reshape(v.shape[:-1] + (-1, 32))
    amax = np.abs(blocks).max(-1, keepdims=True)
    byte = np.maximum(np.where(amax > 0, np.frexp(amax)[1] - 1 + 127, 0) - down, 1)
    scale = np.exp2(byte - 127.0)
    codes = (blocks / scale).astype(np.float32).astype(dtype).astype(np.float64)
    return np.moveaxis((codes * scale).reshape(v.shape), -1, axis)


WIDE = False


def mx_kscale(k):
    if not WIDE:
        return np.ones(k)
    levels = np.array([10, -10, 5, -5, 0])
    if k % 512:
        return np.exp2(np.random.permutation(np.resize(levels, k // 32))).repeat(32)
    a = np.empty((k // 512, 16))
    for p in range(k // 512):
        a[p, :8] = np.random.permutation(np.resize(levels, 8))
        for g in range(8):
            far = levels[np.abs(levels - a[p, g]) >= 10]
            a[p, g + 8] = far[np.random.randint(len(far))]
    return np.exp2(a.ravel()).repeat(32)


def f64(x):
    return np.asarray(x).astype(np.float64)


def striped(idx):
    return np.tile(np.asarray(idx).reshape(-1, 16).T, (8, 1)).astype(np.uint16)


def unstriped(offs):
    return offs[:16].T.reshape(-1).astype(np.int64)


E2M1 = np.array([0.0, 0.5, 1.0, 1.5, 2.0, 3.0, 4.0, 6.0, -0.0, -0.5, -1.0, -1.5, -2.0, -3.0, -4.0, -6.0])


def pack_weight(w, fmt):
    k, n = w.shape
    w = f64(np.asarray(w, np.float32).astype(ml_dtypes.bfloat16)).reshape(k // 32, 32, n)
    amax = np.abs(w).max(1)
    if fmt == "e4m3":
        byte = np.frexp(amax)[1] - 1 + 127 - 7
    else:
        mant, ex = np.frexp(amax / 6.0)
        byte = np.where(mant > 0.5, ex, ex - 1) + 127
    byte = np.clip(np.where(amax > 0, byte, 1), 1, 254)
    scaled = (w * np.exp2(127.0 - byte)[:, None, :]).reshape(k, n).astype(np.float32)
    by_word = np.ascontiguousarray(scaled.reshape(k // 512, 128, 4, n).transpose(0, 1, 3, 2))
    if fmt == "e4m3":
        words = by_word.astype(ml_dtypes.float8_e4m3fn).view(np.uint8)
    else:
        c = by_word.astype(ml_dtypes.float4_e2m1fn).view(np.uint8) & 0xF
        words = (c[..., 0::2] | (c[..., 1::2] << 4)).reshape(k // 512, 128, 2 * n)
    return np.ascontiguousarray(words), np.ascontiguousarray(byte.astype(np.uint8).reshape(k // 512, 16, n))


def unpack_weight(words, scales, fmt):
    g, _, n = scales.shape
    words = np.ascontiguousarray(words).reshape(g, 128, n, -1)
    if fmt == "e4m3":
        vals = words.view(ml_dtypes.float8_e4m3fn).astype(np.float64)
    else:
        nib = np.empty((g, 128, n, 4), np.uint8)
        nib[..., 0::2] = words & 0xF
        nib[..., 1::2] = words >> 4
        vals = E2M1[nib]
    vals = vals * np.repeat(np.exp2(scales.astype(np.float64) - 127.0), 8, axis=1)[..., None]
    return vals.transpose(0, 1, 3, 2).reshape(g * 512, n)


def bf(x):
    return np.asarray(x, np.float32).astype(ml_dtypes.bfloat16)


def planes(Y):
    r, m = Y.shape
    b = f64(bf(Y)).reshape(r // 32, 32, m)
    amax = np.abs(b).max(1)
    byte = np.clip(np.where(amax > 0, np.frexp(amax)[1] - 1 + 127 - 7, 1), 1, 254)
    codes = (b * np.exp2(127.0 - byte)[:, None, :]).reshape(r, m).astype(np.float32).astype(ml_dtypes.float8_e4m3fn).view(np.uint8)
    words = codes.reshape(r // 512, 128, 4, m).transpose(0, 1, 3, 2)
    return np.ascontiguousarray(words), np.ascontiguousarray(byte.astype(np.uint8).reshape(r // 512, 16, m))


D, T, I, Q, E = 512, 2048, 512, 256, 512


def setup_inputs():
    n = np.random.standard_normal
    idx = np.random.permutation(T)[:I]
    fd = mx_kscale(D)
    fi = mx_kscale(I)
    ti = np.ones(T)
    ti[idx] = fi
    keysp = pack_weight(n((D, T)) / fd[:, None], "e2m1")
    return {
        "query": (n((D, Q)) * 0.25 / np.sqrt(D) * fd[:, None]).astype(np.float32),
        "keys_words": keysp[0],
        "keys_scales": keysp[1],
        "age": np.tile(np.random.uniform(0.0, 2.0, T), (128, 1)).astype(np.float32),
        "rate": (np.random.uniform(0.3, 1.2, (Q, 1))).astype(np.float32),
        "reserve": (np.random.uniform(20.0, 100.0, (Q, 1))).astype(np.float32),
        "size": (np.random.uniform(0.5, 2.0, (1, I)) * fi).astype(np.float32),
        "vals": (n((E, T)) / ti).astype(np.float32),
        "offs": striped(idx),
    }


def reference(query, keys_words, keys_scales, age, rate, reserve, size, vals, offs):
    idx = unstriped(offs)
    keysu = unpack_weight(keys_words, keys_scales, "e2m1")
    queryq = mxq(f64(query), 0, "e4m3")
    keysidxg = keysu[:, idx]
    a = queryq.T @ keysidxg
    p = np.exp(a - np.max(a, axis=1, keepdims=True)) * np.exp(f64(age)[:1][:, idx] * f64(rate) * (-1.0))
    w = p * f64(size) / (np.sum(p, axis=1, keepdims=True) + f64(reserve))
    wt = w.T
    vt = f64(vals)[:, idx].T
    vtq = mxq(vt, 0, "e4m3")
    wtq = mxq(wt, 0, "e4m3")
    o = vtq.T @ wtq
    words, scales = planes(o)
    return o, words, scales

@@ -1,0 +1,233 @@
+from contextlib import ExitStack
+
+import concourse.mybir as mybir
+from concourse.masks import make_identity
+
+D, T, I, Q, E = 512, 2048, 512, 256, 512
+FLOPS = 2 * D * Q * I + 2 * I * E * Q
+
+F32 = mybir.dt.float32
+BF16 = mybir.dt.bfloat16
+I32 = mybir.dt.int32
+U32 = mybir.dt.uint32
+U16 = mybir.dt.uint16
+U8 = mybir.dt.uint8
+FP8X4 = mybir.dt.float8_e4m3fn_x4
+FP4X4 = mybir.dt.float4_e2m1fn_x4
+ALU = mybir.AluOpType
+ACT = mybir.ActivationFunctionType
+
+P = 128
+PACK = 4
+HALVES = Q // P
+
+
+def tile_attend_massfade_pl_kernel(
+    tc, query, keys_words, keys_scales, age, rate, reserve, size, vals, offs, out_0, out_1, out_2
+):
+    nc = tc.nc
+    with ExitStack() as ctx:
+        sb = ctx.enter_context(tc.tile_pool(name="sb", bufs=1))
+        ps = ctx.enter_context(tc.psum_pool(name="ps", bufs=1))
+
+        def sbuf(name, shape, dtype):
+            return sb.tile(shape, dtype, name=name, align_bytes=64)
+
+        key_scale_pool = sbuf("key_scale_pool", [P, T], U8)
+        age_pool = sbuf("age_pool", [P, T], F32)
+        nc.vector.memset(key_scale_pool[:].bitcast(I32), 0)
+        nc.vector.memset(age_pool[:], 0.0)
+
+        offsets = sb.tile([P, I // 16], U16, name="offsets")
+        nc.sync.dma_start(offsets[:], offs)
+        key_word_pool = sbuf("key_word_pool", [P, T], U16)
+        nc.sync.dma_start(key_word_pool[:].bitcast(I32), keys_words[0].bitcast(I32))
+        for quad in range(4):
+            nc.sync.dma_start(
+                key_scale_pool[32 * quad : 32 * quad + 4, :].bitcast(I32),
+                keys_scales[0, 4 * quad : 4 * quad + 4, :].bitcast(I32),
+            )
+        nc.sync.dma_start(age_pool[0:1, :], age[0:1, :])
+        query_raw = sbuf("query_raw", [P, PACK, Q], F32)
+        nc.sync.dma_start(query_raw[:], query.rearrange("(p t) q -> p t q", t=PACK))
+        vals_dealt = vals.rearrange("(p t) c -> t p c", t=PACK)
+        val_pools = [sbuf(f"val_pool{t}", [P, T], F32) for t in range(PACK)]
+        for t in range(PACK):
+            nc.sync.dma_start(val_pools[t][:], vals_dealt[t])
+
+        identity = sbuf("identity", [P, P], F32)
+        make_identity(nc, identity[:])
+        small_rows = sbuf("small_rows", [P, P], F32)
+        nc.gpsimd.memset(small_rows[:], 0.0)
+        nc.gpsimd.dma_start(small_rows[0:2, :], rate.rearrange("(h p) o -> h (p o)", p=P))
+        nc.gpsimd.dma_start(small_rows[2:4, :], reserve.rearrange("(h p) o -> h (p o)", p=P))
+        nc.gpsimd.dma_start(small_rows[4:8, :], size.rearrange("o (c p) -> (o c) p", p=P))
+        small_turned = ps.tile([P, P], F32, name="small_turned", tag="val_turned1")
+        nc.tensor.transpose(small_turned[:], small_rows[:], identity[:])
+        small_cols = sbuf("small_cols", [P, 8], F32)
+        nc.scalar.copy(small_cols[:], small_turned[:, 0:8])
+        rate_col, reserve_col, size_col = small_cols[:, 0:2], small_cols[:, 2:4], small_cols[:, 4:8]
+
+        key_words = sbuf("key_words", [P, I], U16)
+        key_scales = sbuf("key_scales", [P, I], U8)
+        age_row = sbuf("age_row", [P, I], F32)
+        nc.vector.tensor_copy(key_words[:], key_word_pool[:].indirect(offsets[:]))
+        nc.vector.tensor_copy(key_scales[:], key_scale_pool[:].indirect(offsets[:]))
+        nc.vector.tensor_copy(age_row[:], age_pool[:].indirect(offsets[:]))
+
+        query_bf = sbuf("query_bf", [P, Q, PACK], BF16)
+        nc.scalar.copy(query_bf[:], query_raw[:].rearrange("p t q -> p q t"))
+        query_codes = sbuf("query_codes", [P, Q], U32)
+        query_scales = sbuf("query_scales", [P, Q], U8)
+        nc.vector.quantize_mx(
+            out=query_codes[:].bitcast(FP8X4),
+            scales=query_scales[:],
+            in_=query_bf[:].rearrange("p q t -> p (q t)"),
+        )
+
+        scores = [ps.tile([P, I], F32, name=f"scores{h}", tag=f"wide{h}") for h in range(HALVES)]
+        for h in range(HALVES):
+            rows = slice(h * P, (h + 1) * P)
+            nc.tensor.matmul_mx(
+                out=scores[h][:],
+                lhsT=query_codes[:, rows].bitcast(FP8X4),
+                lhsT_scale=query_scales[:, rows],
+                rhs=key_words[:].bitcast(FP4X4),
+                rhs_scale=key_scales[:],
+                start=True,
+                stop=True,
+            )
+
+        age_turned = ps.tile([P, PACK, P], F32, name="age_turned", tag="turned")
+        for c in range(PACK):
+            nc.tensor.transpose(age_turned[:, c, :], age_row[:, c * P : (c + 1) * P], identity[:])
+        age_col = sbuf("age_col", [P, PACK], F32)
+        nc.scalar.copy(age_col[:], age_turned[:, :, 0])
+        age_spread = ps.tile([P, PACK, P], F32, name="age_spread")
+        for c in range(PACK):
+            nc.tensor.transpose(age_spread[:, c, :], age_col[:, c : c + 1].to_broadcast([P, P]), identity[:])
+        age_all = sbuf("age_all", [P, I], F32)
+        nc.scalar.copy(age_all[:], age_spread[:].rearrange("p c s -> p (c s)"))
+
+        size_spread = ps.tile([P, PACK, P], F32, name="size_spread")
+        for t in range(PACK):
+            nc.tensor.transpose(size_spread[:, t, :], size_col[:, t : t + 1].to_broadcast([P, P]), identity[:])
+
+        neg_max = [sbuf(f"neg_max{h}", [P, 1], F32) for h in range(HALVES)]
+        fade = [sbuf(f"fade{h}", [P, I], F32) for h in range(HALVES)]
+        prob = [sbuf(f"prob{h}", [P, I], F32) for h in range(HALVES)]
+        row_sum = sbuf("row_sum", [P, HALVES], F32)
+        for h in range(HALVES):
+            nc.vector.tensor_reduce(
+                neg_max[h][:], scores[h][:], mybir.AxisListType.X, ALU.max, negate=True
+            )
+            nc.vector.scalar_tensor_tensor(
+                fade[h][:], age_all[:], rate_col[:, h : h + 1], scores[h][:], ALU.mult, ALU.subtract
+            )
+            nc.scalar.activation(
+                prob[h][:], fade[h][:], ACT.Exp, bias=neg_max[h][:], scale=-1.0,
+                accum_out=row_sum[:, h : h + 1],
+            )
+
+        def gather_values(t):
+            picked = sbuf(f"val_picked{t}", [P, I], BF16)
+            nc.vector.tensor_copy(picked[:], val_pools[t][:].indirect(offsets[:]))
+            words = picked[:].bitcast(F32)
+            turned = ps.tile([P, 2, P], F32, name=f"val_turned{t}", tag=f"val_turned{t % 2}")
+            for u in range(2):
+                nc.tensor.transpose(turned[:, u, :], words[:, u : I // 2 : 2], identity[:])
+            grouped = sbuf(f"val_grouped{t}", [P, P, PACK], BF16)
+            nc.scalar.copy(grouped[:].bitcast(F32), turned[:].rearrange("p u e -> p e u"))
+            return grouped
+
+        def quantise_values(t, grouped):
+            codes = sbuf(f"val_codes{t}", [P, P], U32)
+            scales = sbuf(f"val_scales{t}", [P, P], U8)
+            nc.vector.quantize_mx(
+                out=codes[:].bitcast(FP8X4), scales=scales[:], in_=grouped[:].rearrange("p e t -> p (e t)")
+            )
+            return codes, scales
+
+        val_grouped = [gather_values(t) for t in range(PACK - 1)]
+
+        denom = sbuf("denom", [P, HALVES], F32)
+        inv_denom = sbuf("inv_denom", [P, HALVES], F32)
+        nc.vector.tensor_tensor(denom[:], row_sum[:], reserve_col, ALU.add)
+        nc.vector.reciprocal(inv_denom[:], denom[:])
+        w_turned = ps.tile([P, HALVES, 2, P], F32, name="w_turned", tag="turned")
+        for h in range(HALVES):
+            weight = sbuf(f"weight{h}", [P, I], BF16)
+            nc.vector.scalar_tensor_tensor(
+                weight[:],
+                prob[h][:],
+                inv_denom[:, h : h + 1],
+                size_spread[:].rearrange("p c s -> p (c s)"),
+                ALU.mult,
+                ALU.mult,
+            )
+            words = weight[:].bitcast(F32)
+            for u in range(2):
+                nc.tensor.transpose(w_turned[:, h, u, :], words[:, u : I // 2 : 2], identity[:])
+        w_grouped = sbuf("w_grouped", [P, Q, PACK], BF16)
+        nc.scalar.copy(
+            w_grouped[:].bitcast(F32).rearrange("p (h q) u -> p h q u", h=HALVES),
+            w_turned[:].rearrange("p h u q -> p h q u"),
+        )
+        val_mx = [quantise_values(t, val_grouped[t]) for t in range(PACK - 1)]
+        w_codes = sbuf("w_codes", [P, Q], U32)
+        w_scales = sbuf("w_scales", [P, Q], U8)
+        nc.vector.quantize_mx(
+            out=w_codes[:].bitcast(FP8X4), scales=w_scales[:], in_=w_grouped[:].rearrange("p q t -> p (q t)")
+        )
+        last_grouped = gather_values(PACK - 1)
+
+        result = [ps.tile([P, PACK, P], F32, name=f"result{h}", tag=f"wide{h}") for h in range(HALVES)]
+
+        def multiply(t, codes, scales):
+            for h in range(HALVES):
+                rows = slice(h * P, (h + 1) * P)
+                nc.tensor.matmul_mx(
+                    out=result[h][:, t, :],
+                    lhsT=codes[:].bitcast(FP8X4),
+                    lhsT_scale=scales[:],
+                    rhs=w_codes[:, rows].bitcast(FP8X4),
+                    rhs_scale=w_scales[:, rows],
+                    start=True,
+                    stop=True,
+                )
+
+        out_dealt = out_0.rearrange("(p t) q -> p t q", t=PACK)
+        for t in range(PACK - 1):
+            multiply(t, *val_mx[t])
+        early = sbuf("early", [P, PACK - 1, Q], F32)
+        for h in range(HALVES):
+            nc.scalar.copy(early[:, :, h * P : (h + 1) * P], result[h][:, 0 : PACK - 1, :])
+        nc.sync.dma_start(out_dealt[:, 0 : PACK - 1, :], early[:])
+
+        multiply(PACK - 1, *quantise_values(PACK - 1, last_grouped))
+        result_bf = [sbuf(f"result_bf{h}", [P, P, PACK], BF16) for h in range(HALVES)]
+        nc.vector.tensor_copy(result_bf[0][:], result[0][:].rearrange("p t q -> p q t"))
+        nc.scalar.copy(result_bf[1][:], result[1][:].rearrange("p t q -> p q t"))
+        late = sbuf("late", [P, Q], F32)
+        for h in reversed(range(HALVES)):
+            nc.scalar.copy(late[:, h * P : (h + 1) * P], result[h][:, PACK - 1, :])
+        nc.scalar.dma_start(out_dealt[:, PACK - 1, :], late[:])
+
+        out_codes = sbuf("out_codes", [P, Q], U32)
+        out_scales = sbuf("out_scales", [P, Q], U8)
+        for h in reversed(range(HALVES)):
+            rows = slice(h * P, (h + 1) * P)
+            nc.vector.quantize_mx(
+                out=out_codes[:, rows].bitcast(FP8X4),
+                scales=out_scales[:, rows],
+                in_=result_bf[h][:].rearrange("p q t -> p (q t)"),
+            )
+        nc.sync.dma_start(
+            out_1[0].rearrange("p q t -> p (q t)").bitcast(I32), out_codes[:].bitcast(I32)
+        )
+        for quad in range(4):
+            queue = nc.sync if quad % 2 == 0 else nc.scalar
+            queue.dma_start(
+                out_2[0, 4 * quad : 4 * quad + 4, :].bitcast(I32),
+                out_scales[32 * quad : 32 * quad + 4, :].bitcast(I32),
+            )

@@ -30,43 +30,43 @@ def tile_attend_massfade_pl_kernel(
         sb = ctx.enter_context(tc.tile_pool(name="sb", bufs=1))
         ps = ctx.enter_context(tc.psum_pool(name="ps", bufs=1))
 
-        def sbuf(name, shape, dtype):
-            return sb.tile(shape, dtype, name=name, align_bytes=64)
+        def sbuf(name, shape, dtype, tag=""):
+            return sb.tile(shape, dtype, name=name, tag=tag or name, align_bytes=64)
 
-        key_scale_pool = sbuf("key_scale_pool", [P, T], U8)
+        warm = sbuf("warm", [P, 1], F32)
+        nc.gpsimd.memset(warm[:], 0.0)
+        warm_out = sbuf("warm_out", [P, 1], F32)
+        nc.scalar.activation(warm_out[:], warm[:], ACT.Exp)
+
+        key_scale_pool = sbuf("key_scale_pool", [P, T], U8, tag="pool2")
         age_pool = sbuf("age_pool", [P, T], F32)
+        ones = sbuf("ones", [P, P], F32, tag="pool0")
+        small_rows = sbuf("small_rows", [P, P], F32)
         nc.vector.memset(key_scale_pool[:].bitcast(I32), 0)
-        nc.vector.memset(age_pool[:], 0.0)
+        nc.vector.memset(ones[:], 1.0)
+        nc.vector.memset(age_pool[:].bitcast(I32), 0)
+        nc.vector.memset(small_rows[:], 0.0)
+        identity = sbuf("identity", [P, P], F32)
+        nc.gpsimd.affine_select(
+            out=identity[:], in_=ones[:], compare_op=ALU.is_equal, fill=0.0,
+            base=0, pattern=[[-1, P]], channel_multiplier=1,
+        )
 
         offsets = sb.tile([P, I // 16], U16, name="offsets")
         nc.sync.dma_start(offsets[:], offs)
-        key_word_pool = sbuf("key_word_pool", [P, T], U16)
+        key_word_pool = sbuf("key_word_pool", [P, T], U16, tag="pool1")
         nc.sync.dma_start(key_word_pool[:].bitcast(I32), keys_words[0].bitcast(I32))
+        query_raw = sbuf("query_raw", [P, PACK, Q], F32, tag="pool3")
+        nc.sync.dma_start(query_raw[:], query.rearrange("(p t) q -> p t q", t=PACK))
         for quad in range(4):
-            nc.sync.dma_start(
+            nc.scalar.dma_start(
                 key_scale_pool[32 * quad : 32 * quad + 4, :].bitcast(I32),
                 keys_scales[0, 4 * quad : 4 * quad + 4, :].bitcast(I32),
             )
-        nc.sync.dma_start(age_pool[0:1, :], age[0:1, :])
-        query_raw = sbuf("query_raw", [P, PACK, Q], F32)
-        nc.sync.dma_start(query_raw[:], query.rearrange("(p t) q -> p t q", t=PACK))
-        vals_dealt = vals.rearrange("(p t) c -> t p c", t=PACK)
-        val_pools = [sbuf(f"val_pool{t}", [P, T], F32) for t in range(PACK)]
-        for t in range(PACK):
-            nc.sync.dma_start(val_pools[t][:], vals_dealt[t])
-
-        identity = sbuf("identity", [P, P], F32)
-        make_identity(nc, identity[:])
-        small_rows = sbuf("small_rows", [P, P], F32)
-        nc.gpsimd.memset(small_rows[:], 0.0)
-        nc.gpsimd.dma_start(small_rows[0:2, :], rate.rearrange("(h p) o -> h (p o)", p=P))
-        nc.gpsimd.dma_start(small_rows[2:4, :], reserve.rearrange("(h p) o -> h (p o)", p=P))
-        nc.gpsimd.dma_start(small_rows[4:8, :], size.rearrange("o (c p) -> (o c) p", p=P))
-        small_turned = ps.tile([P, P], F32, name="small_turned", tag="val_turned1")
-        nc.tensor.transpose(small_turned[:], small_rows[:], identity[:])
-        small_cols = sbuf("small_cols", [P, 8], F32)
-        nc.scalar.copy(small_cols[:], small_turned[:, 0:8])
-        rate_col, reserve_col, size_col = small_cols[:, 0:2], small_cols[:, 2:4], small_cols[:, 4:8]
+        nc.scalar.dma_start(age_pool[0:1, :], age[0:1, :])
+        nc.scalar.dma_start(small_rows[0:2, :], rate.rearrange("(h p) o -> h (p o)", p=P))
+        nc.scalar.dma_start(small_rows[2:4, :], reserve.rearrange("(h p) o -> h (p o)", p=P))
+        nc.scalar.dma_start(small_rows[4:8, :], size.rearrange("o (c p) -> (o c) p", p=P))
 
         key_words = sbuf("key_words", [P, I], U16)
         key_scales = sbuf("key_scales", [P, I], U8)
@@ -75,15 +75,17 @@ def tile_attend_massfade_pl_kernel(
         nc.vector.tensor_copy(key_scales[:], key_scale_pool[:].indirect(offsets[:]))
         nc.vector.tensor_copy(age_row[:], age_pool[:].indirect(offsets[:]))
 
-        query_bf = sbuf("query_bf", [P, Q, PACK], BF16)
-        nc.scalar.copy(query_bf[:], query_raw[:].rearrange("p t q -> p q t"))
         query_codes = sbuf("query_codes", [P, Q], U32)
         query_scales = sbuf("query_scales", [P, Q], U8)
-        nc.vector.quantize_mx(
-            out=query_codes[:].bitcast(FP8X4),
-            scales=query_scales[:],
-            in_=query_bf[:].rearrange("p q t -> p (q t)"),
-        )
+        for h in range(HALVES):
+            rows = slice(h * P, (h + 1) * P)
+            query_bf = sbuf(f"query_bf{h}", [P, P, PACK], BF16, tag=("small_cols", "picked0")[h])
+            nc.scalar.copy(query_bf[:], query_raw[:, :, rows].rearrange("p t q -> p q t"))
+            nc.vector.quantize_mx(
+                out=query_codes[:, rows].bitcast(FP8X4),
+                scales=query_scales[:, rows],
+                in_=query_bf[:].rearrange("p q t -> p (q t)"),
+            )
 
         scores = [ps.tile([P, I], F32, name=f"scores{h}", tag=f"wide{h}") for h in range(HALVES)]
         for h in range(HALVES):
@@ -109,12 +111,47 @@ def tile_attend_massfade_pl_kernel(
         age_all = sbuf("age_all", [P, I], F32)
         nc.scalar.copy(age_all[:], age_spread[:].rearrange("p c s -> p (c s)"))
 
+        small_turned = ps.tile([P, P], F32, name="small_turned", tag="turned")
+        nc.tensor.transpose(small_turned[:], small_rows[:], identity[:])
+        small_cols = sbuf("small_cols", [P, 8], F32)
+        nc.scalar.copy(small_cols[:], small_turned[:, 0:8])
+        rate_col, reserve_col, size_col = small_cols[:, 0:2], small_cols[:, 2:4], small_cols[:, 4:8]
+
         size_spread = ps.tile([P, PACK, P], F32, name="size_spread")
         for t in range(PACK):
             nc.tensor.transpose(size_spread[:, t, :], size_col[:, t : t + 1].to_broadcast([P, P]), identity[:])
 
-        neg_max = [sbuf(f"neg_max{h}", [P, 1], F32) for h in range(HALVES)]
-        fade = [sbuf(f"fade{h}", [P, I], F32) for h in range(HALVES)]
+        vals_dealt = vals.rearrange("(p t) c -> t p c", t=PACK)
+        val_pools = [sbuf(f"val_pool{t}", [P, T], F32, tag=f"pool{t}") for t in range(PACK)]
+        for t in range(PACK):
+            nc.sync.dma_start(val_pools[t][:], vals_dealt[t])
+
+        def gather_values(t):
+            picked = sbuf(f"val_picked{t}", [P, I], BF16, tag="pool0" if t == 1 else f"picked{t}")
+            nc.vector.tensor_copy(picked[:], val_pools[t][:].indirect(offsets[:]))
+            return picked
+
+        def turn_values(t, picked):
+            words = picked[:].bitcast(F32)
+            turned = ps.tile([P, 2, P], F32, name=f"val_turned{t}", tag=f"val_turned{t % 2}")
+            for u in range(2):
+                nc.tensor.transpose(turned[:, u, :], words[:, u : I // 2 : 2], identity[:])
+            grouped = sbuf(f"val_grouped{t}", [P, P, PACK], BF16, tag=f"grouped{t}")
+            nc.scalar.copy(grouped[:].bitcast(F32), turned[:].rearrange("p u e -> p e u"))
+            return grouped
+
+        def quantise_values(t, grouped):
+            codes = sbuf(f"val_codes{t}", [P, P], U32, tag=("", "grouped3", "pool3", "")[t])
+            scales = sbuf(f"val_scales{t}", [P, P], U8)
+            nc.vector.quantize_mx(
+                out=codes[:].bitcast(FP8X4), scales=scales[:], in_=grouped[:].rearrange("p e t -> p (e t)")
+            )
+            return codes, scales
+
+        val_grouped = [turn_values(0, gather_values(0))]
+
+        neg_max = [sbuf(f"neg_max{h}", [P, 1], F32, tag=("age_pool", "")[h]) for h in range(HALVES)]
+        fade = [sbuf(f"fade{h}", [P, I], F32, tag=("pool0", "")[h]) for h in range(HALVES)]
         prob = [sbuf(f"prob{h}", [P, I], F32) for h in range(HALVES)]
         row_sum = sbuf("row_sum", [P, HALVES], F32)
         for h in range(HALVES):
@@ -129,34 +166,15 @@ def tile_attend_massfade_pl_kernel(
                 accum_out=row_sum[:, h : h + 1],
             )
 
-        def gather_values(t):
-            picked = sbuf(f"val_picked{t}", [P, I], BF16)
-            nc.vector.tensor_copy(picked[:], val_pools[t][:].indirect(offsets[:]))
-            words = picked[:].bitcast(F32)
-            turned = ps.tile([P, 2, P], F32, name=f"val_turned{t}", tag=f"val_turned{t % 2}")
-            for u in range(2):
-                nc.tensor.transpose(turned[:, u, :], words[:, u : I // 2 : 2], identity[:])
-            grouped = sbuf(f"val_grouped{t}", [P, P, PACK], BF16)
-            nc.scalar.copy(grouped[:].bitcast(F32), turned[:].rearrange("p u e -> p e u"))
-            return grouped
+        val_grouped.append(turn_values(1, gather_values(1)))
 
-        def quantise_values(t, grouped):
-            codes = sbuf(f"val_codes{t}", [P, P], U32)
-            scales = sbuf(f"val_scales{t}", [P, P], U8)
-            nc.vector.quantize_mx(
-                out=codes[:].bitcast(FP8X4), scales=scales[:], in_=grouped[:].rearrange("p e t -> p (e t)")
-            )
-            return codes, scales
-
-        val_grouped = [gather_values(t) for t in range(PACK - 1)]
-
-        denom = sbuf("denom", [P, HALVES], F32)
+        denom = sbuf("denom", [P, HALVES], F32, tag="pool1")
         inv_denom = sbuf("inv_denom", [P, HALVES], F32)
         nc.vector.tensor_tensor(denom[:], row_sum[:], reserve_col, ALU.add)
         nc.vector.reciprocal(inv_denom[:], denom[:])
-        w_turned = ps.tile([P, HALVES, 2, P], F32, name="w_turned", tag="turned")
+        w_grouped = []
         for h in range(HALVES):
-            weight = sbuf(f"weight{h}", [P, I], BF16)
+            weight = sbuf(f"weight{h}", [P, I], BF16, tag=("picked2", "")[h])
             nc.vector.scalar_tensor_tensor(
                 weight[:],
                 prob[h][:],
@@ -166,20 +184,24 @@ def tile_attend_massfade_pl_kernel(
                 ALU.mult,
             )
             words = weight[:].bitcast(F32)
+            w_turned = ps.tile([P, 2, P], F32, name=f"w_turned{h}", tag=("turned", "age_spread")[h])
             for u in range(2):
-                nc.tensor.transpose(w_turned[:, h, u, :], words[:, u : I // 2 : 2], identity[:])
-        w_grouped = sbuf("w_grouped", [P, Q, PACK], BF16)
-        nc.scalar.copy(
-            w_grouped[:].bitcast(F32).rearrange("p (h q) u -> p h q u", h=HALVES),
-            w_turned[:].rearrange("p h u q -> p h q u"),
-        )
-        val_mx = [quantise_values(t, val_grouped[t]) for t in range(PACK - 1)]
-        w_codes = sbuf("w_codes", [P, Q], U32)
+                nc.tensor.transpose(w_turned[:, u, :], words[:, u : I // 2 : 2], identity[:])
+            grouped = sbuf(f"w_grouped{h}", [P, P, PACK], BF16, tag=("picked3", "")[h])
+            nc.scalar.copy(grouped[:].bitcast(F32), w_turned[:].rearrange("p u q -> p q u"))
+            w_grouped.append(grouped)
+        val_grouped.append(turn_values(2, gather_values(2)))
+        w_codes = sbuf("w_codes", [P, Q], U32, tag="pool2")
         w_scales = sbuf("w_scales", [P, Q], U8)
-        nc.vector.quantize_mx(
-            out=w_codes[:].bitcast(FP8X4), scales=w_scales[:], in_=w_grouped[:].rearrange("p q t -> p (q t)")
-        )
-        last_grouped = gather_values(PACK - 1)
+        val_mx = [quantise_values(t, val_grouped[t]) for t in range(2)]
+        for h in range(HALVES):
+            rows = slice(h * P, (h + 1) * P)
+            nc.vector.quantize_mx(
+                out=w_codes[:, rows].bitcast(FP8X4),
+                scales=w_scales[:, rows],
+                in_=w_grouped[h][:].rearrange("p q t -> p (q t)"),
+            )
+        picked = gather_values(PACK - 1)
 
         result = [ps.tile([P, PACK, P], F32, name=f"result{h}", tag=f"wide{h}") for h in range(HALVES)]
 
@@ -197,21 +219,23 @@ def tile_attend_massfade_pl_kernel(
                 )
 
         out_dealt = out_0.rearrange("(p t) q -> p t q", t=PACK)
-        for t in range(PACK - 1):
+        for t in range(2):
             multiply(t, *val_mx[t])
-        early = sbuf("early", [P, PACK - 1, Q], F32)
+        early = sbuf("early", [P, 2, Q], F32)
         for h in range(HALVES):
-            nc.scalar.copy(early[:, :, h * P : (h + 1) * P], result[h][:, 0 : PACK - 1, :])
-        nc.sync.dma_start(out_dealt[:, 0 : PACK - 1, :], early[:])
+            nc.scalar.copy(early[:, :, h * P : (h + 1) * P], result[h][:, 0:2, :])
+        nc.sync.dma_start(out_dealt[:, 0:2, :], early[:])
 
-        multiply(PACK - 1, *quantise_values(PACK - 1, last_grouped))
+        val_grouped.append(turn_values(3, picked))
+        for t in range(2, PACK):
+            multiply(t, *quantise_values(t, val_grouped[t]))
         result_bf = [sbuf(f"result_bf{h}", [P, P, PACK], BF16) for h in range(HALVES)]
         nc.vector.tensor_copy(result_bf[0][:], result[0][:].rearrange("p t q -> p q t"))
         nc.scalar.copy(result_bf[1][:], result[1][:].rearrange("p t q -> p q t"))
-        late = sbuf("late", [P, Q], F32)
+        late = sbuf("late", [P, 2, Q], F32)
         for h in reversed(range(HALVES)):
-            nc.scalar.copy(late[:, h * P : (h + 1) * P], result[h][:, PACK - 1, :])
-        nc.scalar.dma_start(out_dealt[:, PACK - 1, :], late[:])
+            nc.scalar.copy(late[:, :, h * P : (h + 1) * P], result[h][:, 2:PACK, :])
+        nc.scalar.dma_start(out_dealt[:, 2:PACK, :], late[:])
 
         out_codes = sbuf("out_codes", [P, Q], U32)
         out_scales = sbuf("out_scales", [P, Q], U8)

@@ -33,59 +33,60 @@ def tile_attend_massfade_pl_kernel(
         def sbuf(name, shape, dtype, tag=""):
             return sb.tile(shape, dtype, name=name, tag=tag or name, align_bytes=64)
 
-        warm = sbuf("warm", [P, 1], F32)
-        nc.gpsimd.memset(warm[:], 0.0)
-        warm_out = sbuf("warm_out", [P, 1], F32)
-        nc.scalar.activation(warm_out[:], warm[:], ACT.Exp)
-
-        key_scale_pool = sbuf("key_scale_pool", [P, T], U8, tag="pool2")
-        age_pool = sbuf("age_pool", [P, T], F32)
-        ones = sbuf("ones", [P, P], F32, tag="pool0")
-        small_rows = sbuf("small_rows", [P, P], F32)
+        key_scale_pool = sbuf("key_scale_pool", [P, T], U8)
         nc.vector.memset(key_scale_pool[:].bitcast(I32), 0)
-        nc.vector.memset(ones[:], 1.0)
-        nc.vector.memset(age_pool[:].bitcast(I32), 0)
-        nc.vector.memset(small_rows[:], 0.0)
         identity = sbuf("identity", [P, P], F32)
-        nc.gpsimd.affine_select(
-            out=identity[:], in_=ones[:], compare_op=ALU.is_equal, fill=0.0,
-            base=0, pattern=[[-1, P]], channel_multiplier=1,
-        )
+        for half in range(2):
+            ones = sbuf(f"ones{half}", [P, P // 2], F32, tag=("pool2", "small_rows")[half])
+            nc.gpsimd.memset(ones[:], 1.0)
+            nc.gpsimd.affine_select(
+                out=identity[:, half * P // 2 : (half + 1) * P // 2], in_=ones[:],
+                compare_op=ALU.is_equal, fill=0.0,
+                base=-half * P // 2, pattern=[[-1, P // 2]], channel_multiplier=1,
+            )
+        small_rows = sbuf("small_rows", [P, P], F32)
+        nc.gpsimd.memset(small_rows[:], 0.0)
+        warm_out = sbuf("warm_out", [P, 1], F32)
+        warm = sbuf("warm", [P, 1], F32, tag="pool0")
+        nc.gpsimd.memset(warm[:], 0.0)
+        nc.scalar.activation(warm_out[:], warm[:], ACT.Exp)
 
         offsets = sb.tile([P, I // 16], U16, name="offsets")
         nc.sync.dma_start(offsets[:], offs)
-        key_word_pool = sbuf("key_word_pool", [P, T], U16, tag="pool1")
+        key_word_pool = sbuf("key_word_pool", [P, T], U16, tag="key_scales")
         nc.sync.dma_start(key_word_pool[:].bitcast(I32), keys_words[0].bitcast(I32))
-        query_raw = sbuf("query_raw", [P, PACK, Q], F32, tag="pool3")
+        query_raw = sbuf("query_raw", [P, PACK, Q], F32)
         nc.sync.dma_start(query_raw[:], query.rearrange("(p t) q -> p t q", t=PACK))
         for quad in range(4):
-            nc.scalar.dma_start(
+            nc.sync.dma_start(
                 key_scale_pool[32 * quad : 32 * quad + 4, :].bitcast(I32),
                 keys_scales[0, 4 * quad : 4 * quad + 4, :].bitcast(I32),
             )
-        nc.scalar.dma_start(age_pool[0:1, :], age[0:1, :])
-        nc.scalar.dma_start(small_rows[0:2, :], rate.rearrange("(h p) o -> h (p o)", p=P))
-        nc.scalar.dma_start(small_rows[2:4, :], reserve.rearrange("(h p) o -> h (p o)", p=P))
-        nc.scalar.dma_start(small_rows[4:8, :], size.rearrange("o (c p) -> (o c) p", p=P))
+        age_pool = sbuf("age_pool", [P, T], F32, tag="pool2")
+        nc.sync.dma_start(age_pool[:], age)
+        nc.sync.dma_start(small_rows[0:2, :], rate.rearrange("(h p) o -> h (p o)", p=P))
+        nc.sync.dma_start(small_rows[4:8, :], size.rearrange("o (c p) -> (o c) p", p=P))
+        nc.sync.dma_start(small_rows[2:4, :], reserve.rearrange("(h p) o -> h (p o)", p=P))
 
         key_words = sbuf("key_words", [P, I], U16)
-        key_scales = sbuf("key_scales", [P, I], U8)
-        age_row = sbuf("age_row", [P, I], F32)
         nc.vector.tensor_copy(key_words[:], key_word_pool[:].indirect(offsets[:]))
+        key_scales = sbuf("key_scales", [P, I], U8)
         nc.vector.tensor_copy(key_scales[:], key_scale_pool[:].indirect(offsets[:]))
-        nc.vector.tensor_copy(age_row[:], age_pool[:].indirect(offsets[:]))
 
-        query_codes = sbuf("query_codes", [P, Q], U32)
+        query_codes = sbuf("query_codes", [P, Q], U32, tag="pool1")
         query_scales = sbuf("query_scales", [P, Q], U8)
         for h in range(HALVES):
             rows = slice(h * P, (h + 1) * P)
-            query_bf = sbuf(f"query_bf{h}", [P, P, PACK], BF16, tag=("small_cols", "picked0")[h])
+            query_bf = sbuf(f"query_bf{h}", [P, P, PACK], BF16, tag=("small_cols", "pool3")[h])
             nc.scalar.copy(query_bf[:], query_raw[:, :, rows].rearrange("p t q -> p q t"))
             nc.vector.quantize_mx(
                 out=query_codes[:, rows].bitcast(FP8X4),
                 scales=query_scales[:, rows],
                 in_=query_bf[:].rearrange("p q t -> p (q t)"),
             )
+
+        age_all = sbuf("age_all", [P, I], F32, tag="pool3")
+        nc.vector.tensor_copy(age_all[:], age_pool[:].indirect(offsets[:]))
 
         scores = [ps.tile([P, I], F32, name=f"scores{h}", tag=f"wide{h}") for h in range(HALVES)]
         for h in range(HALVES):
@@ -100,18 +101,7 @@ def tile_attend_massfade_pl_kernel(
                 stop=True,
             )
 
-        age_turned = ps.tile([P, PACK, P], F32, name="age_turned", tag="turned")
-        for c in range(PACK):
-            nc.tensor.transpose(age_turned[:, c, :], age_row[:, c * P : (c + 1) * P], identity[:])
-        age_col = sbuf("age_col", [P, PACK], F32)
-        nc.scalar.copy(age_col[:], age_turned[:, :, 0])
-        age_spread = ps.tile([P, PACK, P], F32, name="age_spread")
-        for c in range(PACK):
-            nc.tensor.transpose(age_spread[:, c, :], age_col[:, c : c + 1].to_broadcast([P, P]), identity[:])
-        age_all = sbuf("age_all", [P, I], F32)
-        nc.scalar.copy(age_all[:], age_spread[:].rearrange("p c s -> p (c s)"))
-
-        small_turned = ps.tile([P, P], F32, name="small_turned", tag="turned")
+        small_turned = ps.tile([P, P], F32, name="small_turned", tag="w_turned0")
         nc.tensor.transpose(small_turned[:], small_rows[:], identity[:])
         small_cols = sbuf("small_cols", [P, 8], F32)
         nc.scalar.copy(small_cols[:], small_turned[:, 0:8])
@@ -127,31 +117,41 @@ def tile_attend_massfade_pl_kernel(
             nc.sync.dma_start(val_pools[t][:], vals_dealt[t])
 
         def gather_values(t):
-            picked = sbuf(f"val_picked{t}", [P, I], BF16, tag="pool0" if t == 1 else f"picked{t}")
+            picked = sbuf(f"val_picked{t}", [P, I], BF16, tag=f"picked{t}")
             nc.vector.tensor_copy(picked[:], val_pools[t][:].indirect(offsets[:]))
             return picked
 
+        def cast_values(t):
+            narrow = sbuf(f"val_pool_bf{t}", [P, T], BF16)
+            for c in range(0, T, I):
+                nc.scalar.activation(narrow[:, c : c + I], val_pools[t][:, c : c + I], ACT.Copy)
+            return narrow
+
+        def gather_half_on_scalar(picked, narrow, half):
+            slots = slice(half * I // 2, (half + 1) * I // 2)
+            entries = slice(half * I // 32, (half + 1) * I // 32)
+            nc.scalar.activation(picked[:, slots], narrow[:].indirect(offsets[:, entries]), ACT.Copy)
+
         def turn_values(t, picked):
             words = picked[:].bitcast(F32)
-            turned = ps.tile([P, 2, P], F32, name=f"val_turned{t}", tag=f"val_turned{t % 2}")
+            turned = ps.tile([P, 2, P], F32, name=f"val_turned{t}", tag=f"val_turned{(0, 1, 0, 3)[t]}")
             for u in range(2):
                 nc.tensor.transpose(turned[:, u, :], words[:, u : I // 2 : 2], identity[:])
-            grouped = sbuf(f"val_grouped{t}", [P, P, PACK], BF16, tag=f"grouped{t}")
+            grouped = sbuf(f"val_grouped{t}", [P, P, PACK], BF16)
             nc.scalar.copy(grouped[:].bitcast(F32), turned[:].rearrange("p u e -> p e u"))
             return grouped
 
         def quantise_values(t, grouped):
-            codes = sbuf(f"val_codes{t}", [P, P], U32, tag=("", "grouped3", "pool3", "")[t])
+            codes = sbuf(f"val_codes{t}", [P, P], U32, tag=("", "w_grouped1", "pool1", "")[t])
             scales = sbuf(f"val_scales{t}", [P, P], U8)
             nc.vector.quantize_mx(
                 out=codes[:].bitcast(FP8X4), scales=scales[:], in_=grouped[:].rearrange("p e t -> p (e t)")
             )
             return codes, scales
 
-        val_grouped = [turn_values(0, gather_values(0))]
 
-        neg_max = [sbuf(f"neg_max{h}", [P, 1], F32, tag=("age_pool", "")[h]) for h in range(HALVES)]
-        fade = [sbuf(f"fade{h}", [P, I], F32, tag=("pool0", "")[h]) for h in range(HALVES)]
+        neg_max = [sbuf(f"neg_max{h}", [P, 1], F32) for h in range(HALVES)]
+        fade = [sbuf(f"fade{h}", [P, I], F32, tag=("picked0", "")[h]) for h in range(HALVES)]
         prob = [sbuf(f"prob{h}", [P, I], F32) for h in range(HALVES)]
         row_sum = sbuf("row_sum", [P, HALVES], F32)
         for h in range(HALVES):
@@ -166,15 +166,18 @@ def tile_attend_massfade_pl_kernel(
                 accum_out=row_sum[:, h : h + 1],
             )
 
-        val_grouped.append(turn_values(1, gather_values(1)))
+        val_grouped = {0: turn_values(0, gather_values(0))}
+        narrow = cast_values(1)
+        picked_by_scalar = sbuf("picked_by_scalar", [P, I], BF16)
+        gather_half_on_scalar(picked_by_scalar, narrow, 0)
 
-        denom = sbuf("denom", [P, HALVES], F32, tag="pool1")
+        denom = sbuf("denom", [P, HALVES], F32, tag="pool0")
         inv_denom = sbuf("inv_denom", [P, HALVES], F32)
         nc.vector.tensor_tensor(denom[:], row_sum[:], reserve_col, ALU.add)
         nc.vector.reciprocal(inv_denom[:], denom[:])
         w_grouped = []
         for h in range(HALVES):
-            weight = sbuf(f"weight{h}", [P, I], BF16, tag=("picked2", "")[h])
+            weight = sbuf(f"weight{h}", [P, I], BF16, tag=("picked2", "picked3")[h])
             nc.vector.scalar_tensor_tensor(
                 weight[:],
                 prob[h][:],
@@ -184,16 +187,18 @@ def tile_attend_massfade_pl_kernel(
                 ALU.mult,
             )
             words = weight[:].bitcast(F32)
-            w_turned = ps.tile([P, 2, P], F32, name=f"w_turned{h}", tag=("turned", "age_spread")[h])
+            w_turned = ps.tile([P, 2, P], F32, name=f"w_turned{h}")
             for u in range(2):
                 nc.tensor.transpose(w_turned[:, u, :], words[:, u : I // 2 : 2], identity[:])
-            grouped = sbuf(f"w_grouped{h}", [P, P, PACK], BF16, tag=("picked3", "")[h])
+            grouped = sbuf(f"w_grouped{h}", [P, P, PACK], BF16, tag=("pool1", "")[h])
             nc.scalar.copy(grouped[:].bitcast(F32), w_turned[:].rearrange("p u q -> p q u"))
             w_grouped.append(grouped)
-        val_grouped.append(turn_values(2, gather_values(2)))
-        w_codes = sbuf("w_codes", [P, Q], U32, tag="pool2")
+        gather_half_on_scalar(picked_by_scalar, narrow, 1)
+        val_grouped[2] = turn_values(2, gather_values(2))
+        val_grouped[1] = turn_values(1, picked_by_scalar)
+        val_grouped[3] = turn_values(3, gather_values(3))
+        w_codes = sbuf("w_codes", [P, Q], U32, tag="pool3")
         w_scales = sbuf("w_scales", [P, Q], U8)
-        val_mx = [quantise_values(t, val_grouped[t]) for t in range(2)]
         for h in range(HALVES):
             rows = slice(h * P, (h + 1) * P)
             nc.vector.quantize_mx(
@@ -201,7 +206,7 @@ def tile_attend_massfade_pl_kernel(
                 scales=w_scales[:, rows],
                 in_=w_grouped[h][:].rearrange("p q t -> p (q t)"),
             )
-        picked = gather_values(PACK - 1)
+        val_mx = {t: quantise_values(t, val_grouped[t]) for t in (0, 2, 1, 3)}
 
         result = [ps.tile([P, PACK, P], F32, name=f"result{h}", tag=f"wide{h}") for h in range(HALVES)]
 
@@ -219,23 +224,22 @@ def tile_attend_massfade_pl_kernel(
                 )
 
         out_dealt = out_0.rearrange("(p t) q -> p t q", t=PACK)
-        for t in range(2):
+        for t in (0, 2, 1):
             multiply(t, *val_mx[t])
-        early = sbuf("early", [P, 2, Q], F32)
-        for h in range(HALVES):
-            nc.scalar.copy(early[:, :, h * P : (h + 1) * P], result[h][:, 0:2, :])
-        nc.sync.dma_start(out_dealt[:, 0:2, :], early[:])
+        early = sbuf("early", [P, PACK - 1, P], F32, tag="picked3")
+        nc.scalar.copy(early[:], result[1][:, 0 : PACK - 1, :])
+        nc.sync.dma_start(out_dealt[:, 0 : PACK - 1, P:Q], early[:])
 
-        val_grouped.append(turn_values(3, picked))
-        for t in range(2, PACK):
-            multiply(t, *quantise_values(t, val_grouped[t]))
+        multiply(PACK - 1, *val_mx[PACK - 1])
         result_bf = [sbuf(f"result_bf{h}", [P, P, PACK], BF16) for h in range(HALVES)]
         nc.vector.tensor_copy(result_bf[0][:], result[0][:].rearrange("p t q -> p q t"))
         nc.scalar.copy(result_bf[1][:], result[1][:].rearrange("p t q -> p q t"))
-        late = sbuf("late", [P, 2, Q], F32)
-        for h in reversed(range(HALVES)):
-            nc.scalar.copy(late[:, :, h * P : (h + 1) * P], result[h][:, 2:PACK, :])
-        nc.scalar.dma_start(out_dealt[:, 2:PACK, :], late[:])
+        first_half = sbuf("first_half", [P, PACK, P], F32)
+        nc.scalar.copy(first_half[:], result[0][:])
+        nc.sync.dma_start(out_dealt[:, :, 0:P], first_half[:])
+        late = sbuf("late", [P, P], F32)
+        nc.scalar.copy(late[:], result[1][:, PACK - 1, :])
+        nc.scalar.dma_start(out_dealt[:, PACK - 1, P:Q], late[:])
 
         out_codes = sbuf("out_codes", [P, Q], U32)
         out_scales = sbuf("out_scales", [P, Q], U8)

@@ -1,7 +1,6 @@
 from contextlib import ExitStack
 
 import concourse.mybir as mybir
-from concourse.masks import make_identity
 
 D, T, I, Q, E = 512, 2048, 512, 256, 512
 FLOPS = 2 * D * Q * I + 2 * I * E * Q
@@ -20,6 +19,11 @@ ACT = mybir.ActivationFunctionType
 P = 128
 PACK = 4
 HALVES = Q // P
+QUADS = 4
+STRIP = P // 4
+LIST_ROWS = 16
+ON_SCALAR = 1
+LAST = PACK - 1
 
 
 def tile_attend_massfade_pl_kernel(
@@ -33,36 +37,42 @@ def tile_attend_massfade_pl_kernel(
         def sbuf(name, shape, dtype, tag=""):
             return sb.tile(shape, dtype, name=name, tag=tag or name, align_bytes=64)
 
+
         key_scale_pool = sbuf("key_scale_pool", [P, T], U8)
         nc.vector.memset(key_scale_pool[:].bitcast(I32), 0)
+
         identity = sbuf("identity", [P, P], F32)
-        for half in range(2):
-            ones = sbuf(f"ones{half}", [P, P // 2], F32, tag=("pool2", "small_rows")[half])
+        for strip, tag in enumerate(("slot1", "slot2", "", "small_rows")):
+            first = strip * STRIP
+            ones = sbuf(f"ones{strip}", [P, STRIP], F32, tag=tag)
             nc.gpsimd.memset(ones[:], 1.0)
             nc.gpsimd.affine_select(
-                out=identity[:, half * P // 2 : (half + 1) * P // 2], in_=ones[:],
-                compare_op=ALU.is_equal, fill=0.0,
-                base=-half * P // 2, pattern=[[-1, P // 2]], channel_multiplier=1,
+                out=identity[:, first : first + STRIP],
+                in_=ones[:],
+                compare_op=ALU.is_equal,
+                fill=0.0,
+                base=-first,
+                pattern=[[-1, STRIP]],
+                channel_multiplier=1,
             )
         small_rows = sbuf("small_rows", [P, P], F32)
         nc.gpsimd.memset(small_rows[:], 0.0)
-        warm_out = sbuf("warm_out", [P, 1], F32)
-        warm = sbuf("warm", [P, 1], F32, tag="pool0")
-        nc.gpsimd.memset(warm[:], 0.0)
-        nc.scalar.activation(warm_out[:], warm[:], ACT.Exp)
 
-        offsets = sb.tile([P, I // 16], U16, name="offsets")
+        warm_up = sbuf("warm_up", [P, 1], F32, tag="slot0")
+        nc.scalar.activation(warm_up[:], small_rows[:, 0:1], ACT.Exp)
+
+        offsets = sb.tile([P, I // LIST_ROWS], U16, name="offsets")
         nc.sync.dma_start(offsets[:], offs)
         key_word_pool = sbuf("key_word_pool", [P, T], U16, tag="key_scales")
         nc.sync.dma_start(key_word_pool[:].bitcast(I32), keys_words[0].bitcast(I32))
-        query_raw = sbuf("query_raw", [P, PACK, Q], F32)
-        nc.sync.dma_start(query_raw[:], query.rearrange("(p t) q -> p t q", t=PACK))
-        for quad in range(4):
+        for quad in range(QUADS):
             nc.sync.dma_start(
                 key_scale_pool[32 * quad : 32 * quad + 4, :].bitcast(I32),
                 keys_scales[0, 4 * quad : 4 * quad + 4, :].bitcast(I32),
             )
-        age_pool = sbuf("age_pool", [P, T], F32, tag="pool2")
+        query_raw = sbuf("query_raw", [P, PACK, Q], F32, tag="slot1")
+        nc.sync.dma_start(query_raw[:], query.rearrange("(p t) q -> p t q", t=PACK))
+        age_pool = sbuf("age_pool", [P, T], F32, tag="slot2")
         nc.sync.dma_start(age_pool[:], age)
         nc.sync.dma_start(small_rows[0:2, :], rate.rearrange("(h p) o -> h (p o)", p=P))
         nc.sync.dma_start(small_rows[4:8, :], size.rearrange("o (c p) -> (o c) p", p=P))
@@ -73,20 +83,21 @@ def tile_attend_massfade_pl_kernel(
         key_scales = sbuf("key_scales", [P, I], U8)
         nc.vector.tensor_copy(key_scales[:], key_scale_pool[:].indirect(offsets[:]))
 
-        query_codes = sbuf("query_codes", [P, Q], U32, tag="pool1")
+        query_codes = sbuf("query_codes", [P, Q], U32)
         query_scales = sbuf("query_scales", [P, Q], U8)
         for h in range(HALVES):
             rows = slice(h * P, (h + 1) * P)
-            query_bf = sbuf(f"query_bf{h}", [P, P, PACK], BF16, tag=("small_cols", "pool3")[h])
-            nc.scalar.copy(query_bf[:], query_raw[:, :, rows].rearrange("p t q -> p q t"))
+            query_bf = sbuf(f"query_bf{h}", [P, P, PACK], BF16, tag=("small_cols", "slot3")[h])
+            copy = (nc.scalar.copy, nc.vector.tensor_copy)[h]
+            copy(query_bf[:], query_raw[:, :, rows].rearrange("p t q -> p q t"))
             nc.vector.quantize_mx(
                 out=query_codes[:, rows].bitcast(FP8X4),
                 scales=query_scales[:, rows],
                 in_=query_bf[:].rearrange("p q t -> p (q t)"),
             )
 
-        age_all = sbuf("age_all", [P, I], F32, tag="pool3")
-        nc.vector.tensor_copy(age_all[:], age_pool[:].indirect(offsets[:]))
+        age_picked = sbuf("age_picked", [P, I], F32, tag="slot3")
+        nc.vector.tensor_copy(age_picked[:], age_pool[:].indirect(offsets[:]))
 
         scores = [ps.tile([P, I], F32, name=f"scores{h}", tag=f"wide{h}") for h in range(HALVES)]
         for h in range(HALVES):
@@ -107,12 +118,12 @@ def tile_attend_massfade_pl_kernel(
         nc.scalar.copy(small_cols[:], small_turned[:, 0:8])
         rate_col, reserve_col, size_col = small_cols[:, 0:2], small_cols[:, 2:4], small_cols[:, 4:8]
 
-        size_spread = ps.tile([P, PACK, P], F32, name="size_spread")
-        for t in range(PACK):
-            nc.tensor.transpose(size_spread[:, t, :], size_col[:, t : t + 1].to_broadcast([P, P]), identity[:])
+        size_spread = ps.tile([P, I // P, P], F32, name="size_spread")
+        for c in range(I // P):
+            nc.tensor.transpose(size_spread[:, c, :], size_col[:, c : c + 1].to_broadcast([P, P]), identity[:])
 
         vals_dealt = vals.rearrange("(p t) c -> t p c", t=PACK)
-        val_pools = [sbuf(f"val_pool{t}", [P, T], F32, tag=f"pool{t}") for t in range(PACK)]
+        val_pools = [sbuf(f"val_pool{t}", [P, T], F32, tag=f"slot{t}") for t in range(PACK)]
         for t in range(PACK):
             nc.sync.dma_start(val_pools[t][:], vals_dealt[t])
 
@@ -127,28 +138,30 @@ def tile_attend_massfade_pl_kernel(
                 nc.scalar.activation(narrow[:, c : c + I], val_pools[t][:, c : c + I], ACT.Copy)
             return narrow
 
-        def gather_half_on_scalar(picked, narrow, half):
-            slots = slice(half * I // 2, (half + 1) * I // 2)
-            entries = slice(half * I // 32, (half + 1) * I // 32)
-            nc.scalar.activation(picked[:, slots], narrow[:].indirect(offsets[:, entries]), ACT.Copy)
+        def gather_part_on_scalar(picked, narrow, part):
+            slots = slice(part * I // 2, (part + 1) * I // 2)
+            columns = slice(slots.start // LIST_ROWS, slots.stop // LIST_ROWS)
+            nc.scalar.activation(picked[:, slots], narrow[:].indirect(offsets[:, columns]), ACT.Copy)
 
-        def turn_values(t, picked):
-            words = picked[:].bitcast(F32)
-            turned = ps.tile([P, 2, P], F32, name=f"val_turned{t}", tag=f"val_turned{(0, 1, 0, 3)[t]}")
+        def turn(rounded, turned, grouped):
+            words = rounded[:].bitcast(F32)
             for u in range(2):
                 nc.tensor.transpose(turned[:, u, :], words[:, u : I // 2 : 2], identity[:])
+            nc.scalar.copy(grouped[:].bitcast(F32), turned[:].rearrange("p u r -> p r u"))
+
+        def turn_values(t, picked):
+            turned = ps.tile([P, 2, P], F32, name=f"val_turned{t}", tag=f"val_turned{(0, 1, 0, 3)[t]}")
             grouped = sbuf(f"val_grouped{t}", [P, P, PACK], BF16)
-            nc.scalar.copy(grouped[:].bitcast(F32), turned[:].rearrange("p u e -> p e u"))
+            turn(picked, turned, grouped)
             return grouped
 
         def quantise_values(t, grouped):
-            codes = sbuf(f"val_codes{t}", [P, P], U32, tag=("", "w_grouped1", "pool1", "")[t])
+            codes = sbuf(f"val_codes{t}", [P, P], U32, tag=("", "w_grouped1", "slot1", "")[t])
             scales = sbuf(f"val_scales{t}", [P, P], U8)
             nc.vector.quantize_mx(
                 out=codes[:].bitcast(FP8X4), scales=scales[:], in_=grouped[:].rearrange("p e t -> p (e t)")
             )
             return codes, scales
-
 
         neg_max = [sbuf(f"neg_max{h}", [P, 1], F32) for h in range(HALVES)]
         fade = [sbuf(f"fade{h}", [P, I], F32, tag=("picked0", "")[h]) for h in range(HALVES)]
@@ -159,22 +172,27 @@ def tile_attend_massfade_pl_kernel(
                 neg_max[h][:], scores[h][:], mybir.AxisListType.X, ALU.max, negate=True
             )
             nc.vector.scalar_tensor_tensor(
-                fade[h][:], age_all[:], rate_col[:, h : h + 1], scores[h][:], ALU.mult, ALU.subtract
+                fade[h][:], age_picked[:], rate_col[:, h : h + 1], scores[h][:], ALU.mult, ALU.subtract
             )
             nc.scalar.activation(
-                prob[h][:], fade[h][:], ACT.Exp, bias=neg_max[h][:], scale=-1.0,
+                prob[h][:],
+                fade[h][:],
+                ACT.Exp,
+                bias=neg_max[h][:],
+                scale=-1.0,
                 accum_out=row_sum[:, h : h + 1],
             )
 
         val_grouped = {0: turn_values(0, gather_values(0))}
-        narrow = cast_values(1)
+        narrow = cast_values(ON_SCALAR)
         picked_by_scalar = sbuf("picked_by_scalar", [P, I], BF16)
-        gather_half_on_scalar(picked_by_scalar, narrow, 0)
+        gather_part_on_scalar(picked_by_scalar, narrow, 0)
 
-        denom = sbuf("denom", [P, HALVES], F32, tag="pool0")
+        denom = sbuf("denom", [P, HALVES], F32, tag="slot0")
         inv_denom = sbuf("inv_denom", [P, HALVES], F32)
         nc.vector.tensor_tensor(denom[:], row_sum[:], reserve_col, ALU.add)
         nc.vector.reciprocal(inv_denom[:], denom[:])
+
         w_grouped = []
         for h in range(HALVES):
             weight = sbuf(f"weight{h}", [P, I], BF16, tag=("picked2", "picked3")[h])
@@ -186,18 +204,15 @@ def tile_attend_massfade_pl_kernel(
                 ALU.mult,
                 ALU.mult,
             )
-            words = weight[:].bitcast(F32)
             w_turned = ps.tile([P, 2, P], F32, name=f"w_turned{h}")
-            for u in range(2):
-                nc.tensor.transpose(w_turned[:, u, :], words[:, u : I // 2 : 2], identity[:])
-            grouped = sbuf(f"w_grouped{h}", [P, P, PACK], BF16, tag=("pool1", "")[h])
-            nc.scalar.copy(grouped[:].bitcast(F32), w_turned[:].rearrange("p u q -> p q u"))
-            w_grouped.append(grouped)
-        gather_half_on_scalar(picked_by_scalar, narrow, 1)
+            w_grouped.append(sbuf(f"w_grouped{h}", [P, P, PACK], BF16, tag=("slot1", "")[h]))
+            turn(weight, w_turned, w_grouped[h])
+        gather_part_on_scalar(picked_by_scalar, narrow, 1)
         val_grouped[2] = turn_values(2, gather_values(2))
-        val_grouped[1] = turn_values(1, picked_by_scalar)
-        val_grouped[3] = turn_values(3, gather_values(3))
-        w_codes = sbuf("w_codes", [P, Q], U32, tag="pool3")
+        val_grouped[ON_SCALAR] = turn_values(ON_SCALAR, picked_by_scalar)
+        val_grouped[LAST] = turn_values(LAST, gather_values(LAST))
+
+        w_codes = sbuf("w_codes", [P, Q], U32, tag="slot3")
         w_scales = sbuf("w_scales", [P, Q], U8)
         for h in range(HALVES):
             rows = slice(h * P, (h + 1) * P)
@@ -206,11 +221,12 @@ def tile_attend_massfade_pl_kernel(
                 scales=w_scales[:, rows],
                 in_=w_grouped[h][:].rearrange("p q t -> p (q t)"),
             )
-        val_mx = {t: quantise_values(t, val_grouped[t]) for t in (0, 2, 1, 3)}
+        val_mx = {t: quantise_values(t, val_grouped[t]) for t in val_grouped}
 
         result = [ps.tile([P, PACK, P], F32, name=f"result{h}", tag=f"wide{h}") for h in range(HALVES)]
 
-        def multiply(t, codes, scales):
+        def multiply(t):
+            codes, scales = val_mx[t]
             for h in range(HALVES):
                 rows = slice(h * P, (h + 1) * P)
                 nc.tensor.matmul_mx(
@@ -224,13 +240,13 @@ def tile_attend_massfade_pl_kernel(
                 )
 
         out_dealt = out_0.rearrange("(p t) q -> p t q", t=PACK)
-        for t in (0, 2, 1):
-            multiply(t, *val_mx[t])
-        early = sbuf("early", [P, PACK - 1, P], F32, tag="picked3")
-        nc.scalar.copy(early[:], result[1][:, 0 : PACK - 1, :])
-        nc.sync.dma_start(out_dealt[:, 0 : PACK - 1, P:Q], early[:])
+        for t in (0, 2, ON_SCALAR):
+            multiply(t)
+        early = sbuf("early", [P, LAST, P], F32, tag="picked3")
+        nc.scalar.copy(early[:], result[1][:, 0:LAST, :])
+        nc.sync.dma_start(out_dealt[:, 0:LAST, P:Q], early[:])
+        multiply(LAST)
 
-        multiply(PACK - 1, *val_mx[PACK - 1])
         result_bf = [sbuf(f"result_bf{h}", [P, P, PACK], BF16) for h in range(HALVES)]
         nc.vector.tensor_copy(result_bf[0][:], result[0][:].rearrange("p t q -> p q t"))
         nc.scalar.copy(result_bf[1][:], result[1][:].rearrange("p t q -> p q t"))
@@ -238,8 +254,8 @@ def tile_attend_massfade_pl_kernel(
         nc.scalar.copy(first_half[:], result[0][:])
         nc.sync.dma_start(out_dealt[:, :, 0:P], first_half[:])
         late = sbuf("late", [P, P], F32)
-        nc.scalar.copy(late[:], result[1][:, PACK - 1, :])
-        nc.scalar.dma_start(out_dealt[:, PACK - 1, P:Q], late[:])
+        nc.scalar.copy(late[:], result[1][:, LAST, :])
+        nc.scalar.dma_start(out_dealt[:, LAST, P:Q], late[:])
 
         out_codes = sbuf("out_codes", [P, Q], U32)
         out_scales = sbuf("out_scales", [P, Q], U8)
@@ -250,10 +266,8 @@ def tile_attend_massfade_pl_kernel(
                 scales=out_scales[:, rows],
                 in_=result_bf[h][:].rearrange("p q t -> p (q t)"),
             )
-        nc.sync.dma_start(
-            out_1[0].rearrange("p q t -> p (q t)").bitcast(I32), out_codes[:].bitcast(I32)
-        )
-        for quad in range(4):
+        nc.sync.dma_start(out_1[0].rearrange("p q t -> p (q t)").bitcast(I32), out_codes[:].bitcast(I32))
+        for quad in range(QUADS):
             queue = nc.sync if quad % 2 == 0 else nc.scalar
             queue.dma_start(
                 out_2[0, 4 * quad : 4 * quad + 4, :].bitcast(I32),

from contextlib import ExitStack

import concourse.mybir as mybir

D, T, I, Q, E = 512, 2048, 512, 256, 512
FLOPS = 2 * D * Q * I + 2 * I * E * Q

F32 = mybir.dt.float32
BF16 = mybir.dt.bfloat16
I32 = mybir.dt.int32
U32 = mybir.dt.uint32
U16 = mybir.dt.uint16
U8 = mybir.dt.uint8
FP8X4 = mybir.dt.float8_e4m3fn_x4
FP4X4 = mybir.dt.float4_e2m1fn_x4
ALU = mybir.AluOpType
ACT = mybir.ActivationFunctionType

P = 128
PACK = 4
HALVES = Q // P
QUADS = 4
STRIP = P // 4
LIST_ROWS = 16
ON_SCALAR = 1
LAST = PACK - 1


def tile_attend_massfade_pl_kernel(
    tc, query, keys_words, keys_scales, age, rate, reserve, size, vals, offs, out_0, out_1, out_2
):
    nc = tc.nc
    with ExitStack() as ctx:
        sb = ctx.enter_context(tc.tile_pool(name="sb", bufs=1))
        ps = ctx.enter_context(tc.psum_pool(name="ps", bufs=1))

        def sbuf(name, shape, dtype, tag=""):
            return sb.tile(shape, dtype, name=name, tag=tag or name, align_bytes=64)


        key_scale_pool = sbuf("key_scale_pool", [P, T], U8)
        nc.vector.memset(key_scale_pool[:].bitcast(I32), 0)

        identity = sbuf("identity", [P, P], F32)
        for strip, tag in enumerate(("slot1", "slot2", "", "small_rows")):
            first = strip * STRIP
            ones = sbuf(f"ones{strip}", [P, STRIP], F32, tag=tag)
            nc.gpsimd.memset(ones[:], 1.0)
            nc.gpsimd.affine_select(
                out=identity[:, first : first + STRIP],
                in_=ones[:],
                compare_op=ALU.is_equal,
                fill=0.0,
                base=-first,
                pattern=[[-1, STRIP]],
                channel_multiplier=1,
            )
        small_rows = sbuf("small_rows", [P, P], F32)
        nc.gpsimd.memset(small_rows[:], 0.0)

        warm_up = sbuf("warm_up", [P, 1], F32, tag="slot0")
        nc.scalar.activation(warm_up[:], small_rows[:, 0:1], ACT.Exp)

        offsets = sb.tile([P, I // LIST_ROWS], U16, name="offsets")
        nc.sync.dma_start(offsets[:], offs)
        key_word_pool = sbuf("key_word_pool", [P, T], U16, tag="key_scales")
        nc.sync.dma_start(key_word_pool[:].bitcast(I32), keys_words[0].bitcast(I32))
        for quad in range(QUADS):
            nc.sync.dma_start(
                key_scale_pool[32 * quad : 32 * quad + 4, :].bitcast(I32),
                keys_scales[0, 4 * quad : 4 * quad + 4, :].bitcast(I32),
            )
        query_raw = sbuf("query_raw", [P, PACK, Q], F32, tag="slot1")
        nc.sync.dma_start(query_raw[:], query.rearrange("(p t) q -> p t q", t=PACK))
        age_pool = sbuf("age_pool", [P, T], F32, tag="slot2")
        nc.sync.dma_start(age_pool[:], age)
        nc.sync.dma_start(small_rows[0:2, :], rate.rearrange("(h p) o -> h (p o)", p=P))
        nc.sync.dma_start(small_rows[4:8, :], size.rearrange("o (c p) -> (o c) p", p=P))
        nc.sync.dma_start(small_rows[2:4, :], reserve.rearrange("(h p) o -> h (p o)", p=P))

        key_words = sbuf("key_words", [P, I], U16)
        nc.vector.tensor_copy(key_words[:], key_word_pool[:].indirect(offsets[:]))
        key_scales = sbuf("key_scales", [P, I], U8)
        nc.vector.tensor_copy(key_scales[:], key_scale_pool[:].indirect(offsets[:]))

        query_codes = sbuf("query_codes", [P, Q], U32)
        query_scales = sbuf("query_scales", [P, Q], U8)
        for h in range(HALVES):
            rows = slice(h * P, (h + 1) * P)
            query_bf = sbuf(f"query_bf{h}", [P, P, PACK], BF16, tag=("small_cols", "slot3")[h])
            copy = (nc.scalar.copy, nc.vector.tensor_copy)[h]
            copy(query_bf[:], query_raw[:, :, rows].rearrange("p t q -> p q t"))
            nc.vector.quantize_mx(
                out=query_codes[:, rows].bitcast(FP8X4),
                scales=query_scales[:, rows],
                in_=query_bf[:].rearrange("p q t -> p (q t)"),
            )

        age_picked = sbuf("age_picked", [P, I], F32, tag="slot3")
        nc.vector.tensor_copy(age_picked[:], age_pool[:].indirect(offsets[:]))

        scores = [ps.tile([P, I], F32, name=f"scores{h}", tag=f"wide{h}") for h in range(HALVES)]
        for h in range(HALVES):
            rows = slice(h * P, (h + 1) * P)
            nc.tensor.matmul_mx(
                out=scores[h][:],
                lhsT=query_codes[:, rows].bitcast(FP8X4),
                lhsT_scale=query_scales[:, rows],
                rhs=key_words[:].bitcast(FP4X4),
                rhs_scale=key_scales[:],
                start=True,
                stop=True,
            )

        small_turned = ps.tile([P, P], F32, name="small_turned", tag="w_turned0")
        nc.tensor.transpose(small_turned[:], small_rows[:], identity[:])
        small_cols = sbuf("small_cols", [P, 8], F32)
        nc.scalar.copy(small_cols[:], small_turned[:, 0:8])
        rate_col, reserve_col, size_col = small_cols[:, 0:2], small_cols[:, 2:4], small_cols[:, 4:8]

        size_spread = ps.tile([P, I // P, P], F32, name="size_spread")
        for c in range(I // P):
            nc.tensor.transpose(size_spread[:, c, :], size_col[:, c : c + 1].to_broadcast([P, P]), identity[:])

        vals_dealt = vals.rearrange("(p t) c -> t p c", t=PACK)
        val_pools = [sbuf(f"val_pool{t}", [P, T], F32, tag=f"slot{t}") for t in range(PACK)]
        for t in range(PACK):
            nc.sync.dma_start(val_pools[t][:], vals_dealt[t])

        def gather_values(t):
            picked = sbuf(f"val_picked{t}", [P, I], BF16, tag=f"picked{t}")
            nc.vector.tensor_copy(picked[:], val_pools[t][:].indirect(offsets[:]))
            return picked

        def cast_values(t):
            narrow = sbuf(f"val_pool_bf{t}", [P, T], BF16)
            for c in range(0, T, I):
                nc.scalar.activation(narrow[:, c : c + I], val_pools[t][:, c : c + I], ACT.Copy)
            return narrow

        def gather_part_on_scalar(picked, narrow, part):
            slots = slice(part * I // 2, (part + 1) * I // 2)
            columns = slice(slots.start // LIST_ROWS, slots.stop // LIST_ROWS)
            nc.scalar.activation(picked[:, slots], narrow[:].indirect(offsets[:, columns]), ACT.Copy)

        def turn(rounded, turned, grouped):
            words = rounded[:].bitcast(F32)
            for u in range(2):
                nc.tensor.transpose(turned[:, u, :], words[:, u : I // 2 : 2], identity[:])
            nc.scalar.copy(grouped[:].bitcast(F32), turned[:].rearrange("p u r -> p r u"))

        def turn_values(t, picked):
            turned = ps.tile([P, 2, P], F32, name=f"val_turned{t}", tag=f"val_turned{(0, 1, 0, 3)[t]}")
            grouped = sbuf(f"val_grouped{t}", [P, P, PACK], BF16)
            turn(picked, turned, grouped)
            return grouped

        def quantise_values(t, grouped):
            codes = sbuf(f"val_codes{t}", [P, P], U32, tag=("", "w_grouped1", "slot1", "")[t])
            scales = sbuf(f"val_scales{t}", [P, P], U8)
            nc.vector.quantize_mx(
                out=codes[:].bitcast(FP8X4), scales=scales[:], in_=grouped[:].rearrange("p e t -> p (e t)")
            )
            return codes, scales

        neg_max = [sbuf(f"neg_max{h}", [P, 1], F32) for h in range(HALVES)]
        fade = [sbuf(f"fade{h}", [P, I], F32, tag=("picked0", "")[h]) for h in range(HALVES)]
        prob = [sbuf(f"prob{h}", [P, I], F32) for h in range(HALVES)]
        row_sum = sbuf("row_sum", [P, HALVES], F32)
        for h in range(HALVES):
            nc.vector.tensor_reduce(
                neg_max[h][:], scores[h][:], mybir.AxisListType.X, ALU.max, negate=True
            )
            nc.vector.scalar_tensor_tensor(
                fade[h][:], age_picked[:], rate_col[:, h : h + 1], scores[h][:], ALU.mult, ALU.subtract
            )
            nc.scalar.activation(
                prob[h][:],
                fade[h][:],
                ACT.Exp,
                bias=neg_max[h][:],
                scale=-1.0,
                accum_out=row_sum[:, h : h + 1],
            )

        val_grouped = {0: turn_values(0, gather_values(0))}
        narrow = cast_values(ON_SCALAR)
        picked_by_scalar = sbuf("picked_by_scalar", [P, I], BF16)
        gather_part_on_scalar(picked_by_scalar, narrow, 0)

        denom = sbuf("denom", [P, HALVES], F32, tag="slot0")
        inv_denom = sbuf("inv_denom", [P, HALVES], F32)
        nc.vector.tensor_tensor(denom[:], row_sum[:], reserve_col, ALU.add)
        nc.vector.reciprocal(inv_denom[:], denom[:])

        w_grouped = []
        for h in range(HALVES):
            weight = sbuf(f"weight{h}", [P, I], BF16, tag=("picked2", "picked3")[h])
            nc.vector.scalar_tensor_tensor(
                weight[:],
                prob[h][:],
                inv_denom[:, h : h + 1],
                size_spread[:].rearrange("p c s -> p (c s)"),
                ALU.mult,
                ALU.mult,
            )
            w_turned = ps.tile([P, 2, P], F32, name=f"w_turned{h}")
            w_grouped.append(sbuf(f"w_grouped{h}", [P, P, PACK], BF16, tag=("slot1", "")[h]))
            turn(weight, w_turned, w_grouped[h])
        gather_part_on_scalar(picked_by_scalar, narrow, 1)
        val_grouped[2] = turn_values(2, gather_values(2))
        val_grouped[ON_SCALAR] = turn_values(ON_SCALAR, picked_by_scalar)
        val_grouped[LAST] = turn_values(LAST, gather_values(LAST))

        w_codes = sbuf("w_codes", [P, Q], U32, tag="slot3")
        w_scales = sbuf("w_scales", [P, Q], U8)
        for h in range(HALVES):
            rows = slice(h * P, (h + 1) * P)
            nc.vector.quantize_mx(
                out=w_codes[:, rows].bitcast(FP8X4),
                scales=w_scales[:, rows],
                in_=w_grouped[h][:].rearrange("p q t -> p (q t)"),
            )
        val_mx = {t: quantise_values(t, val_grouped[t]) for t in val_grouped}

        result = [ps.tile([P, PACK, P], F32, name=f"result{h}", tag=f"wide{h}") for h in range(HALVES)]

        def multiply(t):
            codes, scales = val_mx[t]
            for h in range(HALVES):
                rows = slice(h * P, (h + 1) * P)
                nc.tensor.matmul_mx(
                    out=result[h][:, t, :],
                    lhsT=codes[:].bitcast(FP8X4),
                    lhsT_scale=scales[:],
                    rhs=w_codes[:, rows].bitcast(FP8X4),
                    rhs_scale=w_scales[:, rows],
                    start=True,
                    stop=True,
                )

        out_dealt = out_0.rearrange("(p t) q -> p t q", t=PACK)
        for t in (0, 2, ON_SCALAR):
            multiply(t)
        early = sbuf("early", [P, LAST, P], F32, tag="picked3")
        nc.scalar.copy(early[:], result[1][:, 0:LAST, :])
        nc.sync.dma_start(out_dealt[:, 0:LAST, P:Q], early[:])
        multiply(LAST)

        result_bf = [sbuf(f"result_bf{h}", [P, P, PACK], BF16) for h in range(HALVES)]
        nc.vector.tensor_copy(result_bf[0][:], result[0][:].rearrange("p t q -> p q t"))
        nc.scalar.copy(result_bf[1][:], result[1][:].rearrange("p t q -> p q t"))
        first_half = sbuf("first_half", [P, PACK, P], F32)
        nc.scalar.copy(first_half[:], result[0][:])
        nc.sync.dma_start(out_dealt[:, :, 0:P], first_half[:])
        late = sbuf("late", [P, P], F32)
        nc.scalar.copy(late[:], result[1][:, LAST, :])
        nc.scalar.dma_start(out_dealt[:, LAST, P:Q], late[:])

        out_codes = sbuf("out_codes", [P, Q], U32)
        out_scales = sbuf("out_scales", [P, Q], U8)
        for h in reversed(range(HALVES)):
            rows = slice(h * P, (h + 1) * P)
            nc.vector.quantize_mx(
                out=out_codes[:, rows].bitcast(FP8X4),
                scales=out_scales[:, rows],
                in_=result_bf[h][:].rearrange("p q t -> p (q t)"),
            )
        nc.sync.dma_start(out_1[0].rearrange("p q t -> p (q t)").bitcast(I32), out_codes[:].bitcast(I32))
        for quad in range(QUADS):
            queue = nc.sync if quad % 2 == 0 else nc.scalar
            queue.dma_start(
                out_2[0, 4 * quad : 4 * quad + 4, :].bitcast(I32),
                out_scales[32 * quad : 32 * quad + 4, :].bitcast(I32),
            )
